import numpy as np, ml_dtypes
CORES = [34,162,290,418,42,426]
N = 6
TK = 512
COEF = [[2,-1,0,1,0,-1],[-1,2,-1,0,1,0],[0,-1,2,-1,0,1],[1,0,-1,2,-1,0],[0,1,0,-1,2,-1],[-1,0,1,0,-1,2]]
def setup_inputs(rng):
    return {"x": rng.standard_normal((N, 128, TK), dtype=np.float32).astype(ml_dtypes.bfloat16), "a": (rng.standard_normal((N, 128, 128), dtype=np.float32) / 11).astype(ml_dtypes.bfloat16)}
def setup_inputs_big(rng):
    d = setup_inputs(rng)
    for k in ("x", "a"): d[k] = (d[k].astype(np.float32) * 1024.0).astype(d[k].dtype)
    return d
def setup_inputs_small(rng):
    d = setup_inputs(rng)
    for k in ("x", "a"): d[k] = (d[k].astype(np.float32) * (1 / 1024.0)).astype(d[k].dtype)
    return d
def setup_inputs_apart(rng):
    d = setup_inputs(rng)
    f = (10.0 ** rng.permutation(np.linspace(-1.5, 1.5, N))).astype(np.float32).reshape(N, 1, 1)
    for k in ("x", "a"): d[k] = (d[k].astype(np.float32) * f).astype(d[k].dtype)
    return d
def reference(x, a):
    X, A = x.astype(np.float64), a.astype(np.float64)
    y = np.stack([A[r].T @ sum(COEF[r][j] * X[j] for j in range(N)) for r in range(N)])
    return {"y": y.astype(ml_dtypes.bfloat16)}

@@ -1,0 +1,96 @@
+from concourse.bass import DstId, RemoteDMATransfer
+from concourse.mybir import AluOpType
+
+TK = 512
+HALF = TK // 2
+NSRC = 3
+
+SCRATCH = {
+    "xs": ("sbuf", [128, TK], "bfloat16"),
+    "land": ("sbuf", [128, NSRC * TK], "bfloat16"),
+    "a1": ("sbuf", [128, 128], "bfloat16"),
+    "a2": ("sbuf", [128, 128], "bfloat16"),
+    "an": ("sbuf", [128, 128], "bfloat16"),
+    "ys": ("sbuf", [128, TK], "bfloat16"),
+    "p0": ("psum", [128, TK], "float32"),
+    "p1": ("psum", [128, TK], "float32"),
+}
+SEMAPHORES = ["xin", "ain", "prep", "sent", "mm0", "mm1", "cast", "out"] + ["from%d" % j for j in range(6)]
+
+
+def _way(topo, s, d):
+    crosses = topo.rack(topo.host(s)) != topo.rack(topo.host(d))
+    if crosses:
+        one = topo.chip(s) == topo.chip(d)
+    else:
+        one = topo.mates(s, d) or topo.same_plane(s, d)
+    return (1 if one else 2, 1 if crosses else 0)
+
+
+def rank_program(g, core, T, topo):
+    rank = T.rank_of(core)
+    if rank is None:
+        return
+    coef = T.tables["COEF"]
+    n = len(T.cores)
+    sem = T.sem
+
+    def takers(j):
+        rs = [r for r in range(n) if r != j and coef[r][j] != 0]
+        return sorted(rs, key=lambda r: _way(topo, T.cores[j], T.cores[r]))
+
+    def sources(r):
+        js = [j for j in range(n) if j != r and coef[r][j] != 0]
+        return sorted(js, key=lambda j: (takers(j).index(r), j))
+
+    g.sync.dma_start(T.xs[:], T.x[:]).then_inc(sem.xin, 16)
+    g.scalar.dma_start(T.a1[:], T.a[:]).then_inc(sem.ain, 16)
+
+    dests = takers(rank)
+    mask = topo.mask(core, T.cores[dests[0]])
+    for r in dests:
+        mask &= topo.mask(core, T.cores[r])
+    engines = bin(mask).count("1")
+    ids, dsts = [], []
+    for r in dests:
+        rid, pid = topo.addr(T.cores[r], core)
+        k = sources(r).index(rank)
+        ids.append(DstId(rid=rid, pnc=pid))
+        dsts.append(T.land[:, k * TK:(k + 1) * TK])
+    g.wait_ge(sem.xin, 16)
+    g.remote_dma_fused(
+        [RemoteDMATransfer(dst_ids=ids, dma_engine_mask=mask, remote_sem=sem["from%d" % rank], srcs=[T.xs[:]], dsts=dsts,
+                           alu_op=0)],
+        local_sem=sem.sent)
+
+    v = g.vector
+    v.wait_ge(sem.ain, 16)
+    v.tensor_tensor(T.a2[:], T.a1[:], T.a1[:], AluOpType.add).then_inc(sem.prep, 1)
+    v.wait_ge(sem.prep, 1)
+    v.tensor_tensor(T.an[:], T.a1[:], T.a2[:], AluOpType.subtract).then_inc(sem.prep, 1)
+
+    weight = {1: T.a1, 2: T.a2, -1: T.an}
+    banks = (T.p0, T.p1)
+    done = (sem.mm0, sem.mm1)
+    t = g.tensor
+    t.wait_ge(sem.prep, 2)
+    t.wait_ge(sem.xin, 16)
+    for h in range(2):
+        t.matmul(banks[h][:, 0:HALF], weight[coef[rank][rank]][:], T.xs[:, h * HALF:(h + 1) * HALF], True, False)
+    srcs = sources(rank)
+    for k, j in enumerate(srcs):
+        last = k == len(srcs) - 1
+        t.wait_ge(sem["from%d" % j], engines)
+        for h in range(2):
+            m = t.matmul(banks[h][:, 0:HALF], weight[coef[rank][j]][:],
+                         T.land[:, k * TK + h * HALF:k * TK + (h + 1) * HALF], False, last)
+            if last:
+                m.then_inc(done[h], 1)
+
+    for h in range(2):
+        v.wait_ge(done[h], 1)
+        v.tensor_copy(T.ys[:, h * HALF:(h + 1) * HALF], banks[h][:, 0:HALF]).then_inc(sem.cast, 1)
+    g.sync.wait_ge(sem.cast, 2)
+    g.sync.dma_start(T.y[:], T.ys[:]).then_inc(sem.out, 16)
+    g.sync.wait_ge(sem.out, 16)
+    g.wait_ge(sem.sent, engines)

@@ -41,27 +41,32 @@ def rank_program(g, core, T, topo):
 
     def sources(r):
         js = [j for j in range(n) if j != r and coef[r][j] != 0]
-        return sorted(js, key=lambda j: (takers(j).index(r), j))
+        return sorted(js, key=lambda j: (_way(topo, T.cores[j], T.cores[r]), j))
+
+    def engines_of(j):
+        rs = takers(j)
+        mask = topo.mask(T.cores[j], T.cores[rs[0]])
+        for r in rs:
+            mask &= topo.mask(T.cores[j], T.cores[r])
+        bits = [b for b in range(16) if (mask >> b) & 1]
+        half = len(bits) // 2
+        cable = [r for r in rs if _way(topo, T.cores[j], T.cores[r]) == (1, 1)][0]
+        rest = [r for r in rs if r != cable]
+        return {rest[0]: bits[0:half:2], cable: bits[1:half:2], rest[1]: bits[half::2]}
 
     g.sync.dma_start(T.xs[:], T.x[:]).then_inc(sem.xin, 16)
-    g.scalar.dma_start(T.a1[:], T.a[:]).then_inc(sem.ain, 16)
+    g.sync.dma_start(T.a1[:], T.a[:]).then_inc(sem.ain, 16)
 
-    dests = takers(rank)
-    mask = topo.mask(core, T.cores[dests[0]])
-    for r in dests:
-        mask &= topo.mask(core, T.cores[r])
-    engines = bin(mask).count("1")
-    ids, dsts = [], []
-    for r in dests:
+    mine = engines_of(rank)
+    transfers = []
+    for r in takers(rank):
         rid, pid = topo.addr(T.cores[r], core)
         k = sources(r).index(rank)
-        ids.append(DstId(rid=rid, pnc=pid))
-        dsts.append(T.land[:, k * TK:(k + 1) * TK])
+        transfers.append(RemoteDMATransfer(dst_ids=[DstId(rid=rid, pnc=pid)], dma_engine_mask=sum(1 << b for b in mine[r]),
+                                           remote_sem=sem["from%d" % rank], src=T.xs[:],
+                                           dst=T.land[:, k * TK:(k + 1) * TK], alu_op=0))
     g.wait_ge(sem.xin, 16)
-    g.remote_dma_fused(
-        [RemoteDMATransfer(dst_ids=ids, dma_engine_mask=mask, remote_sem=sem["from%d" % rank], srcs=[T.xs[:]], dsts=dsts,
-                           alu_op=0)],
-        local_sem=sem.sent)
+    g.remote_dma_fused(transfers, local_sem=sem.sent)
 
     v = g.vector
     v.wait_ge(sem.ain, 16)
@@ -80,7 +85,7 @@ def rank_program(g, core, T, topo):
     srcs = sources(rank)
     for k, j in enumerate(srcs):
         last = k == len(srcs) - 1
-        t.wait_ge(sem["from%d" % j], engines)
+        t.wait_ge(sem["from%d" % j], len(engines_of(j)[rank]))
         for h in range(2):
             m = t.matmul(banks[h][:, 0:HALF], weight[coef[rank][j]][:],
                          T.land[:, k * TK + h * HALF:k * TK + (h + 1) * HALF], False, last)
@@ -93,4 +98,4 @@ def rank_program(g, core, T, topo):
     g.sync.wait_ge(sem.cast, 2)
     g.sync.dma_start(T.y[:], T.ys[:]).then_inc(sem.out, 16)
     g.sync.wait_ge(sem.out, 16)
-    g.wait_ge(sem.sent, engines)
+    g.wait_ge(sem.sent, sum(len(e) for e in mine.values()))

@@ -2,8 +2,10 @@ from concourse.bass import DstId, RemoteDMATransfer
 from concourse.mybir import AluOpType
 
 TK = 512
-HALF = TK // 2
+PARTS = 2
+W = TK // PARTS
 NSRC = 3
+WORLD = 512
 
 SCRATCH = {
     "xs": ("sbuf", [128, TK], "bfloat16"),
@@ -15,7 +17,8 @@ SCRATCH = {
     "p0": ("psum", [128, TK], "float32"),
     "p1": ("psum", [128, TK], "float32"),
 }
-SEMAPHORES = ["xin", "ain", "prep", "sent", "mm0", "mm1", "cast", "out"] + ["from%d" % j for j in range(6)]
+SEMAPHORES = (["ain", "prep", "sent", "hin"] + ["%s%d" % (s, h) for s in ("xin", "mm", "cast", "out") for h in range(PARTS)]
+              + ["from%d_%d" % (j, h) for j in range(6) for h in range(PARTS)])
 
 
 def _way(topo, s, d):
@@ -27,46 +30,96 @@ def _way(topo, s, d):
     return (1 if one else 2, 1 if crosses else 0)
 
 
+def _bits(mask):
+    return [b for b in range(16) if (mask >> b) & 1]
+
+
+def _mask(bits):
+    return sum(1 << b for b in bits)
+
+
 def rank_program(g, core, T, topo):
-    rank = T.rank_of(core)
-    if rank is None:
-        return
     coef = T.tables["COEF"]
-    n = len(T.cores)
+    cores = T.cores
+    n = len(cores)
     sem = T.sem
+    cols = [slice(h * W, (h + 1) * W) for h in range(PARTS)]
+
+    def way(j, r):
+        return _way(topo, cores[j], cores[r])
 
     def takers(j):
-        rs = [r for r in range(n) if r != j and coef[r][j] != 0]
-        return sorted(rs, key=lambda r: _way(topo, T.cores[j], T.cores[r]))
+        return sorted([r for r in range(n) if r != j and coef[r][j] != 0], key=lambda r: way(j, r))
+
+    def handed(j):
+        far = [r for r in takers(j) if way(j, r)[1]]
+        alone = [r for r in far if way(j, r)[0] == 1]
+        return alone[0] if len(far) > 1 and alone else None
+
+    def helpers(j):
+        c = cores[j]
+        chip = [h for h in range(WORLD) if h != c and topo.host(h) == topo.host(c) and topo.chip(h) == topo.chip(c)]
+        across = [h for h in range(WORLD) if topo.mates(c, h)][0]
+        near = [h for h in chip if topo.die(h) == topo.die(c) and not topo.may_write(h, across)]
+        other = [h for h in chip if topo.die(h) != topo.die(c)]
+        return [near[0], other[0]]
 
     def sources(r):
-        js = [j for j in range(n) if j != r and coef[r][j] != 0]
-        return sorted(js, key=lambda j: (_way(topo, T.cores[j], T.cores[r]), j))
+        return sorted([j for j in range(n) if j != r and coef[r][j] != 0], key=lambda j: (way(j, r), j))
+
+    def landing(r, j, h):
+        k = sources(r).index(j)
+        return T.land[:, k * TK + h * W:k * TK + (h + 1) * W]
 
     def engines_of(j):
         rs = takers(j)
-        mask = topo.mask(T.cores[j], T.cores[rs[0]])
+        mask = topo.mask(cores[j], cores[rs[0]])
         for r in rs:
-            mask &= topo.mask(T.cores[j], T.cores[r])
-        bits = [b for b in range(16) if (mask >> b) & 1]
+            mask &= topo.mask(cores[j], cores[r])
+        bits = _bits(mask)
         half = len(bits) // 2
-        cable = [r for r in rs if _way(topo, T.cores[j], T.cores[r]) == (1, 1)][0]
-        rest = [r for r in rs if r != cable]
-        return {rest[0]: bits[0:half:2], cable: bits[1:half:2], rest[1]: bits[half::2]}
+        rest = [bits[0:half:2], bits[half::2]]
+        return {r: bits[1:half:2] if way(j, r) == (1, 1) else rest.pop(0) for r in rs}
 
-    g.sync.dma_start(T.xs[:], T.x[:]).then_inc(sem.xin, 16)
-    g.sync.dma_start(T.a1[:], T.a[:]).then_inc(sem.ain, 16)
+    for j in range(n):
+        if handed(j) is not None and core in helpers(j):
+            h = helpers(j).index(core)
+            r = handed(j)
+            rid, pid = topo.addr(cores[r], core)
+            out = _bits(topo.mask(core, cores[r]))[0:4:2]
+            g.wait_ge(sem.hin, 4)
+            g.remote_dma(landing(r, j, h), T.xs[:, cols[h]], sem["from%d_%d" % (j, h)], sem.sent, pid, rid, _mask(out))
+            g.wait_ge(sem.sent, len(out))
+            return
+
+    rank = T.rank_of(core)
+    if rank is None:
+        return
+    queues = (g.sync, g.scalar)
+
+    for h in range(PARTS):
+        queues[h].dma_start(T.xs[:, cols[h]], T.x[:, cols[h]]).then_inc(sem["xin%d" % h], 16)
+    g.scalar.dma_start(T.a1[:], T.a[:]).then_inc(sem.ain, 16)
 
     mine = engines_of(rank)
-    transfers = []
-    for r in takers(rank):
-        rid, pid = topo.addr(T.cores[r], core)
-        k = sources(r).index(rank)
-        transfers.append(RemoteDMATransfer(dst_ids=[DstId(rid=rid, pnc=pid)], dma_engine_mask=sum(1 << b for b in mine[r]),
-                                           remote_sem=sem["from%d" % rank], src=T.xs[:],
-                                           dst=T.land[:, k * TK:(k + 1) * TK], alu_op=0))
-    g.wait_ge(sem.xin, 16)
-    g.remote_dma_fused(transfers, local_sem=sem.sent)
+    sent = 0
+    for h in range(PARTS):
+        transfers = []
+        for r in takers(rank):
+            if r == handed(rank):
+                to = helpers(rank)[h]
+                leaving = topo.mask(core, cores[r])
+                eng = [b for b in _bits(topo.mask(core, to)) if not (leaving >> b) & 1][0:8:2]
+                dst, arrived = T.xs[:, cols[h]], sem.hin
+            else:
+                to, eng = cores[r], mine[r]
+                dst, arrived = landing(r, rank, h), sem["from%d_%d" % (rank, h)]
+            rid, pid = topo.addr(to, core)
+            transfers.append(RemoteDMATransfer(dst_ids=[DstId(rid=rid, pnc=pid)], dma_engine_mask=_mask(eng),
+                                               remote_sem=arrived, src=T.xs[:, cols[h]], dst=dst, alu_op=0))
+            sent += len(eng)
+        g.wait_ge(sem["xin%d" % h], 16)
+        g.remote_dma_fused(transfers, local_sem=sem.sent)
 
     v = g.vector
     v.wait_ge(sem.ain, 16)
@@ -76,26 +129,23 @@ def rank_program(g, core, T, topo):
 
     weight = {1: T.a1, 2: T.a2, -1: T.an}
     banks = (T.p0, T.p1)
-    done = (sem.mm0, sem.mm1)
     t = g.tensor
     t.wait_ge(sem.prep, 2)
-    t.wait_ge(sem.xin, 16)
-    for h in range(2):
-        t.matmul(banks[h][:, 0:HALF], weight[coef[rank][rank]][:], T.xs[:, h * HALF:(h + 1) * HALF], True, False)
-    srcs = sources(rank)
-    for k, j in enumerate(srcs):
-        last = k == len(srcs) - 1
-        t.wait_ge(sem["from%d" % j], len(engines_of(j)[rank]))
-        for h in range(2):
-            m = t.matmul(banks[h][:, 0:HALF], weight[coef[rank][j]][:],
-                         T.land[:, k * TK + h * HALF:k * TK + (h + 1) * HALF], False, last)
-            if last:
-                m.then_inc(done[h], 1)
+    for h in range(PARTS):
+        t.wait_ge(sem["xin%d" % h], 16)
+        t.matmul(banks[h][:, 0:W], weight[coef[rank][rank]][:], T.xs[:, cols[h]], True, False)
+    blocks = sorted([(handed(j) == rank, h, k, j) for k, j in enumerate(sources(rank)) for h in range(PARTS)])
+    for i, (_, h, k, j) in enumerate(blocks):
+        last = all(b[1] != h for b in blocks[i + 1:])
+        t.wait_ge(sem["from%d_%d" % (j, h)], 2)
+        m = t.matmul(banks[h][:, 0:W], weight[coef[rank][j]][:], landing(rank, j, h), False, last)
+        if last:
+            m.then_inc(sem["mm%d" % h], 1)
 
-    for h in range(2):
-        v.wait_ge(done[h], 1)
-        v.tensor_copy(T.ys[:, h * HALF:(h + 1) * HALF], banks[h][:, 0:HALF]).then_inc(sem.cast, 1)
-    g.sync.wait_ge(sem.cast, 2)
-    g.sync.dma_start(T.y[:], T.ys[:]).then_inc(sem.out, 16)
-    g.sync.wait_ge(sem.out, 16)
-    g.wait_ge(sem.sent, sum(len(e) for e in mine.values()))
+    for h in range(PARTS):
+        v.wait_ge(sem["mm%d" % h], 1)
+        v.tensor_copy(T.ys[:, cols[h]], banks[h][:, 0:W]).then_inc(sem["cast%d" % h], 1)
+        queues[h].wait_ge(sem["cast%d" % h], 1)
+        queues[h].dma_start(T.y[:, cols[h]], T.ys[:, cols[h]]).then_inc(sem["out%d" % h], 16)
+        queues[h].wait_ge(sem["out%d" % h], 16)
+    g.wait_ge(sem.sent, sent)

@@ -2,13 +2,18 @@ from concourse.bass import DstId, RemoteDMATransfer
 from concourse.mybir import AluOpType
 
 TK = 512
-PARTS = 2
-W = TK // PARTS
+W = TK // 2
+Q = TK // 4
 NSRC = 3
 WORLD = 512
+PIECE = [slice(0, W), slice(W, TK), slice(W, W + Q), slice(W + Q, TK)]
+SEGS = [slice(0, W), slice(W, W + Q), slice(W + Q, TK)]
+COVERS = [[0], [1, 2], [1], [2]]
 
 SCRATCH = {
     "xs": ("sbuf", [128, TK], "bfloat16"),
+    "xd": ("dram", [2, 128, W], "bfloat16"),
+    "xq": ("dram", [128, Q], "bfloat16"),
     "land": ("sbuf", [128, NSRC * TK], "bfloat16"),
     "a1": ("sbuf", [128, 128], "bfloat16"),
     "a2": ("sbuf", [128, 128], "bfloat16"),
@@ -16,9 +21,11 @@ SCRATCH = {
     "ys": ("sbuf", [128, TK], "bfloat16"),
     "p0": ("psum", [128, TK], "float32"),
     "p1": ("psum", [128, TK], "float32"),
+    "p2": ("psum", [128, TK], "float32"),
 }
-SEMAPHORES = (["ain", "prep", "sent", "hin"] + ["%s%d" % (s, h) for s in ("xin", "mm", "cast", "out") for h in range(PARTS)]
-              + ["from%d_%d" % (j, h) for j in range(6) for h in range(PARTS)])
+SEMAPHORES = (["ain", "prep", "sent", "hin", "xqin", "xin0", "xin1", "xd0", "xd1", "out0", "out1"]
+              + ["%s%d" % (s, k) for s in ("mm", "cast") for k in range(3)]
+              + ["from%d_%d" % (j, p) for j in range(6) for p in range(4)])
 
 
 def _way(topo, s, d):
@@ -43,7 +50,6 @@ def rank_program(g, core, T, topo):
     cores = T.cores
     n = len(cores)
     sem = T.sem
-    cols = [slice(h * W, (h + 1) * W) for h in range(PARTS)]
 
     def way(j, r):
         return _way(topo, cores[j], cores[r])
@@ -56,20 +62,24 @@ def rank_program(g, core, T, topo):
         alone = [r for r in far if way(j, r)[0] == 1]
         return alone[0] if len(far) > 1 and alone else None
 
+    def kept(j):
+        return [r for r in takers(j) if way(j, r)[1] and r != handed(j)][0]
+
     def helpers(j):
         c = cores[j]
         chip = [h for h in range(WORLD) if h != c and topo.host(h) == topo.host(c) and topo.chip(h) == topo.chip(c)]
         across = [h for h in range(WORLD) if topo.mates(c, h)][0]
         near = [h for h in chip if topo.die(h) == topo.die(c) and not topo.may_write(h, across)]
-        other = [h for h in chip if topo.die(h) != topo.die(c)]
-        return [near[0], other[0]]
+        plain = [h for h in chip if topo.die(h) != topo.die(c) and not topo.may_write(h, across)]
+        port = [h for h in chip if topo.die(h) != topo.die(c) and topo.may_write(h, across)]
+        return [near[0], plain[0], port[0]]
 
     def sources(r):
         return sorted([j for j in range(n) if j != r and coef[r][j] != 0], key=lambda j: (way(j, r), j))
 
-    def landing(r, j, h):
+    def landing(r, j, cols):
         k = sources(r).index(j)
-        return T.land[:, k * TK + h * W:k * TK + (h + 1) * W]
+        return T.land[:, k * TK + cols.start:k * TK + cols.stop]
 
     def engines_of(j):
         rs = takers(j)
@@ -82,13 +92,19 @@ def rank_program(g, core, T, topo):
         return {r: bits[1:half:2] if way(j, r) == (1, 1) else rest.pop(0) for r in rs}
 
     for j in range(n):
-        if handed(j) is not None and core in helpers(j):
-            h = helpers(j).index(core)
-            r = handed(j)
+        hs = helpers(j)
+        if core in hs:
+            i = hs.index(core)
+            if i < 2:
+                r, piece, src = handed(j), i, T.xd[i]
+                if r is None:
+                    return
+            else:
+                r, piece, src = kept(j), 3, T.xq[:]
             rid, pid = topo.addr(cores[r], core)
             out = _bits(topo.mask(core, cores[r]))[0:4:2]
             g.wait_ge(sem.hin, 4)
-            g.remote_dma(landing(r, j, h), T.xs[:, cols[h]], sem["from%d_%d" % (j, h)], sem.sent, pid, rid, _mask(out))
+            g.remote_dma(landing(r, j, PIECE[piece]), src, sem["from%d_%d" % (j, piece)], sem.sent, pid, rid, _mask(out))
             g.wait_ge(sem.sent, len(out))
             return
 
@@ -96,30 +112,46 @@ def rank_program(g, core, T, topo):
     if rank is None:
         return
     queues = (g.sync, g.scalar)
+    hand, keep, helper = handed(rank), kept(rank), helpers(rank)
 
-    for h in range(PARTS):
-        queues[h].dma_start(T.xs[:, cols[h]], T.x[:, cols[h]]).then_inc(sem["xin%d" % h], 16)
+    if hand is not None:
+        for h in range(2):
+            queues[h].dma_start(T.xd[h], T.x[:, PIECE[h]]).then_inc(sem["xd%d" % h], 16)
+        g.sync.dma_start(T.xs[:, PIECE[1]], T.x[:, PIECE[1]]).then_inc(sem.xin1, 16)
+        g.scalar.dma_start(T.xq[:], T.x[:, PIECE[3]]).then_inc(sem.xqin, 16)
+        g.sync.dma_start(T.xs[:, PIECE[0]], T.x[:, PIECE[0]]).then_inc(sem.xin0, 16)
+    else:
+        for h in range(2):
+            queues[h].dma_start(T.xs[:, PIECE[h]], T.x[:, PIECE[h]]).then_inc(sem["xin%d" % h], 16)
+        g.sync.dma_start(T.xq[:], T.x[:, PIECE[3]]).then_inc(sem.xqin, 16)
     g.scalar.dma_start(T.a1[:], T.a[:]).then_inc(sem.ain, 16)
 
     mine = engines_of(rank)
-    sent = 0
-    for h in range(PARTS):
+    leaving = topo.mask(core, cores[keep])
+    inside = [b for b in _bits(topo.mask(core, helper[0])) if not (leaving >> b) & 1][0:8:2]
+    sent = [0]
+
+    def transfer(to, eng, src, dst, arrived):
+        rid, pid = topo.addr(to, core)
+        sent[0] += len(eng)
+        return RemoteDMATransfer(dst_ids=[DstId(rid=rid, pnc=pid)], dma_engine_mask=_mask(eng), remote_sem=arrived,
+                                 src=src, dst=dst, alu_op=0)
+
+    for h in range(2):
+        src = T.xd[h] if hand is not None else T.xs[:, PIECE[h]]
         transfers = []
         for r in takers(rank):
-            if r == handed(rank):
-                to = helpers(rank)[h]
-                leaving = topo.mask(core, cores[r])
-                eng = [b for b in _bits(topo.mask(core, to)) if not (leaving >> b) & 1][0:8:2]
-                dst, arrived = T.xs[:, cols[h]], sem.hin
-            else:
-                to, eng = cores[r], mine[r]
-                dst, arrived = landing(r, rank, h), sem["from%d_%d" % (rank, h)]
-            rid, pid = topo.addr(to, core)
-            transfers.append(RemoteDMATransfer(dst_ids=[DstId(rid=rid, pnc=pid)], dma_engine_mask=_mask(eng),
-                                               remote_sem=arrived, src=T.xs[:, cols[h]], dst=dst, alu_op=0))
-            sent += len(eng)
-        g.wait_ge(sem["xin%d" % h], 16)
+            if r == hand:
+                transfers.append(transfer(helper[h], inside, src, T.xd[h], sem.hin))
+            elif r != keep or h == 0:
+                transfers.append(transfer(cores[r], mine[r], src, landing(r, rank, PIECE[h]), sem["from%d_%d" % (rank, h)]))
+        g.wait_ge(sem["xd%d" % h] if hand is not None else sem["xin%d" % h], 16)
         g.remote_dma_fused(transfers, local_sem=sem.sent)
+    g.wait_ge(sem.xin1, 16)
+    g.wait_ge(sem.xqin, 16)
+    g.remote_dma_fused([transfer(cores[keep], mine[keep], T.xs[:, PIECE[2]], landing(keep, rank, PIECE[2]),
+                                 sem["from%d_2" % rank]),
+                        transfer(helper[2], inside, T.xq[:], T.xq[:], sem.hin)], local_sem=sem.sent)
 
     v = g.vector
     v.wait_ge(sem.ain, 16)
@@ -128,24 +160,43 @@ def rank_program(g, core, T, topo):
     v.tensor_tensor(T.an[:], T.a1[:], T.a2[:], AluOpType.subtract).then_inc(sem.prep, 1)
 
     weight = {1: T.a1, 2: T.a2, -1: T.an}
-    banks = (T.p0, T.p1)
+    banks = (T.p0, T.p1, T.p2)
+
+    def bank(s):
+        return banks[s][:, 0:SEGS[s].stop - SEGS[s].start]
+
     t = g.tensor
     t.wait_ge(sem.prep, 2)
-    for h in range(PARTS):
-        t.wait_ge(sem["xin%d" % h], 16)
-        t.matmul(banks[h][:, 0:W], weight[coef[rank][rank]][:], T.xs[:, cols[h]], True, False)
-    blocks = sorted([(handed(j) == rank, h, k, j) for k, j in enumerate(sources(rank)) for h in range(PARTS)])
-    for i, (_, h, k, j) in enumerate(blocks):
-        last = all(b[1] != h for b in blocks[i + 1:])
-        t.wait_ge(sem["from%d_%d" % (j, h)], 2)
-        m = t.matmul(banks[h][:, 0:W], weight[coef[rank][j]][:], landing(rank, j, h), False, last)
+    t.wait_ge(sem.xin0, 16)
+    t.wait_ge(sem.xin1, 16)
+    for s in range(3):
+        t.matmul(bank(s), weight[coef[rank][rank]][:], T.xs[:, SEGS[s]], True, False)
+    events = []
+    for j in sources(rank):
+        if handed(j) == rank:
+            events += [(4, j, 0), (6, j, 1)]
+        elif kept(j) == rank:
+            events += [(1, j, 0), (3, j, 2), (5, j, 3)]
+        else:
+            events += [(0, j, 0), (2, j, 1)]
+    events.sort()
+    work = [(j, p, s) for _, j, p in events for s in COVERS[p]]
+    waited = set()
+    for i, (j, p, s) in enumerate(work):
+        if (j, p) not in waited:
+            waited.add((j, p))
+            t.wait_ge(sem["from%d_%d" % (j, p)], 2)
+        last = all(w[2] != s for w in work[i + 1:])
+        m = t.matmul(bank(s), weight[coef[rank][j]][:], landing(rank, j, SEGS[s]), False, last)
         if last:
-            m.then_inc(sem["mm%d" % h], 1)
+            m.then_inc(sem["mm%d" % s], 1)
 
-    for h in range(PARTS):
-        v.wait_ge(sem["mm%d" % h], 1)
-        v.tensor_copy(T.ys[:, cols[h]], banks[h][:, 0:W]).then_inc(sem["cast%d" % h], 1)
-        queues[h].wait_ge(sem["cast%d" % h], 1)
-        queues[h].dma_start(T.y[:, cols[h]], T.ys[:, cols[h]]).then_inc(sem["out%d" % h], 16)
+    for s in range(3):
+        v.wait_ge(sem["mm%d" % s], 1)
+        v.tensor_copy(T.ys[:, SEGS[s]], bank(s)).then_inc(sem["cast%d" % s], 1)
+    for h in range(2):
+        for s in COVERS[h]:
+            queues[h].wait_ge(sem["cast%d" % s], 1)
+        queues[h].dma_start(T.y[:, PIECE[h]], T.ys[:, PIECE[h]]).then_inc(sem["out%d" % h], 16)
         queues[h].wait_ge(sem["out%d" % h], 16)
-    g.wait_ge(sem.sent, sent)
+    g.wait_ge(sem.sent, sent[0])

from concourse.bass import DstId, RemoteDMATransfer
from concourse.mybir import AluOpType

TK = 512
W = TK // 2
Q = TK // 4
NSRC = 3
WORLD = 512
PIECE = [slice(0, W), slice(W, TK), slice(W, W + Q), slice(W + Q, TK)]
SEGS = [slice(0, W), slice(W, W + Q), slice(W + Q, TK)]
COVERS = [[0], [1, 2], [1], [2]]

SCRATCH = {
    "xs": ("sbuf", [128, TK], "bfloat16"),
    "xd": ("dram", [2, 128, W], "bfloat16"),
    "xq": ("dram", [128, Q], "bfloat16"),
    "land": ("sbuf", [128, NSRC * TK], "bfloat16"),
    "a1": ("sbuf", [128, 128], "bfloat16"),
    "a2": ("sbuf", [128, 128], "bfloat16"),
    "an": ("sbuf", [128, 128], "bfloat16"),
    "ys": ("sbuf", [128, TK], "bfloat16"),
    "p0": ("psum", [128, TK], "float32"),
    "p1": ("psum", [128, TK], "float32"),
    "p2": ("psum", [128, TK], "float32"),
}
SEMAPHORES = (["ain", "prep", "sent", "hin", "xqin", "xin0", "xin1", "xd0", "xd1", "out0", "out1"]
              + ["%s%d" % (s, k) for s in ("mm", "cast") for k in range(3)]
              + ["from%d_%d" % (j, p) for j in range(6) for p in range(4)])


def _way(topo, s, d):
    crosses = topo.rack(topo.host(s)) != topo.rack(topo.host(d))
    if crosses:
        one = topo.chip(s) == topo.chip(d)
    else:
        one = topo.mates(s, d) or topo.same_plane(s, d)
    return (1 if one else 2, 1 if crosses else 0)


def _bits(mask):
    return [b for b in range(16) if (mask >> b) & 1]


def _mask(bits):
    return sum(1 << b for b in bits)


def rank_program(g, core, T, topo):
    coef = T.tables["COEF"]
    cores = T.cores
    n = len(cores)
    sem = T.sem

    def way(j, r):
        return _way(topo, cores[j], cores[r])

    def takers(j):
        return sorted([r for r in range(n) if r != j and coef[r][j] != 0], key=lambda r: way(j, r))

    def handed(j):
        far = [r for r in takers(j) if way(j, r)[1]]
        alone = [r for r in far if way(j, r)[0] == 1]
        return alone[0] if len(far) > 1 and alone else None

    def kept(j):
        return [r for r in takers(j) if way(j, r)[1] and r != handed(j)][0]

    def helpers(j):
        c = cores[j]
        chip = [h for h in range(WORLD) if h != c and topo.host(h) == topo.host(c) and topo.chip(h) == topo.chip(c)]
        across = [h for h in range(WORLD) if topo.mates(c, h)][0]
        near = [h for h in chip if topo.die(h) == topo.die(c) and not topo.may_write(h, across)]
        plain = [h for h in chip if topo.die(h) != topo.die(c) and not topo.may_write(h, across)]
        port = [h for h in chip if topo.die(h) != topo.die(c) and topo.may_write(h, across)]
        return [near[0], plain[0], port[0]]

    def sources(r):
        return sorted([j for j in range(n) if j != r and coef[r][j] != 0], key=lambda j: (way(j, r), j))

    def landing(r, j, cols):
        k = sources(r).index(j)
        return T.land[:, k * TK + cols.start:k * TK + cols.stop]

    def engines_of(j):
        rs = takers(j)
        mask = topo.mask(cores[j], cores[rs[0]])
        for r in rs:
            mask &= topo.mask(cores[j], cores[r])
        bits = _bits(mask)
        half = len(bits) // 2
        rest = [bits[0:half:2], bits[half::2]]
        return {r: bits[1:half:2] if way(j, r) == (1, 1) else rest.pop(0) for r in rs}

    for j in range(n):
        hs = helpers(j)
        if core in hs:
            i = hs.index(core)
            if i < 2:
                r, piece, src = handed(j), i, T.xd[i]
                if r is None:
                    return
            else:
                r, piece, src = kept(j), 3, T.xq[:]
            rid, pid = topo.addr(cores[r], core)
            out = _bits(topo.mask(core, cores[r]))[0:4:2]
            g.wait_ge(sem.hin, 4)
            g.remote_dma(landing(r, j, PIECE[piece]), src, sem["from%d_%d" % (j, piece)], sem.sent, pid, rid, _mask(out))
            g.wait_ge(sem.sent, len(out))
            return

    rank = T.rank_of(core)
    if rank is None:
        return
    queues = (g.sync, g.scalar)
    hand, keep, helper = handed(rank), kept(rank), helpers(rank)

    if hand is not None:
        for h in range(2):
            queues[h].dma_start(T.xd[h], T.x[:, PIECE[h]]).then_inc(sem["xd%d" % h], 16)
        g.sync.dma_start(T.xs[:, PIECE[1]], T.x[:, PIECE[1]]).then_inc(sem.xin1, 16)
        g.scalar.dma_start(T.xq[:], T.x[:, PIECE[3]]).then_inc(sem.xqin, 16)
        g.sync.dma_start(T.xs[:, PIECE[0]], T.x[:, PIECE[0]]).then_inc(sem.xin0, 16)
    else:
        for h in range(2):
            queues[h].dma_start(T.xs[:, PIECE[h]], T.x[:, PIECE[h]]).then_inc(sem["xin%d" % h], 16)
        g.sync.dma_start(T.xq[:], T.x[:, PIECE[3]]).then_inc(sem.xqin, 16)
    g.scalar.dma_start(T.a1[:], T.a[:]).then_inc(sem.ain, 16)

    mine = engines_of(rank)
    leaving = topo.mask(core, cores[keep])
    inside = [b for b in _bits(topo.mask(core, helper[0])) if not (leaving >> b) & 1][0:8:2]
    sent = [0]

    def transfer(to, eng, src, dst, arrived):
        rid, pid = topo.addr(to, core)
        sent[0] += len(eng)
        return RemoteDMATransfer(dst_ids=[DstId(rid=rid, pnc=pid)], dma_engine_mask=_mask(eng), remote_sem=arrived,
                                 src=src, dst=dst, alu_op=0)

    for h in range(2):
        src = T.xd[h] if hand is not None else T.xs[:, PIECE[h]]
        transfers = []
        for r in takers(rank):
            if r == hand:
                transfers.append(transfer(helper[h], inside, src, T.xd[h], sem.hin))
            elif r != keep or h == 0:
                transfers.append(transfer(cores[r], mine[r], src, landing(r, rank, PIECE[h]), sem["from%d_%d" % (rank, h)]))
        g.wait_ge(sem["xd%d" % h] if hand is not None else sem["xin%d" % h], 16)
        g.remote_dma_fused(transfers, local_sem=sem.sent)
    g.wait_ge(sem.xin1, 16)
    g.wait_ge(sem.xqin, 16)
    g.remote_dma_fused([transfer(cores[keep], mine[keep], T.xs[:, PIECE[2]], landing(keep, rank, PIECE[2]),
                                 sem["from%d_2" % rank]),
                        transfer(helper[2], inside, T.xq[:], T.xq[:], sem.hin)], local_sem=sem.sent)

    v = g.vector
    v.wait_ge(sem.ain, 16)
    v.tensor_tensor(T.a2[:], T.a1[:], T.a1[:], AluOpType.add).then_inc(sem.prep, 1)
    v.wait_ge(sem.prep, 1)
    v.tensor_tensor(T.an[:], T.a1[:], T.a2[:], AluOpType.subtract).then_inc(sem.prep, 1)

    weight = {1: T.a1, 2: T.a2, -1: T.an}
    banks = (T.p0, T.p1, T.p2)

    def bank(s):
        return banks[s][:, 0:SEGS[s].stop - SEGS[s].start]

    t = g.tensor
    t.wait_ge(sem.prep, 2)
    t.wait_ge(sem.xin0, 16)
    t.wait_ge(sem.xin1, 16)
    for s in range(3):
        t.matmul(bank(s), weight[coef[rank][rank]][:], T.xs[:, SEGS[s]], True, False)
    events = []
    for j in sources(rank):
        if handed(j) == rank:
            events += [(4, j, 0), (6, j, 1)]
        elif kept(j) == rank:
            events += [(1, j, 0), (3, j, 2), (5, j, 3)]
        else:
            events += [(0, j, 0), (2, j, 1)]
    events.sort()
    work = [(j, p, s) for _, j, p in events for s in COVERS[p]]
    waited = set()
    for i, (j, p, s) in enumerate(work):
        if (j, p) not in waited:
            waited.add((j, p))
            t.wait_ge(sem["from%d_%d" % (j, p)], 2)
        last = all(w[2] != s for w in work[i + 1:])
        m = t.matmul(bank(s), weight[coef[rank][j]][:], landing(rank, j, SEGS[s]), False, last)
        if last:
            m.then_inc(sem["mm%d" % s], 1)

    for s in range(3):
        v.wait_ge(sem["mm%d" % s], 1)
        v.tensor_copy(T.ys[:, SEGS[s]], bank(s)).then_inc(sem["cast%d" % s], 1)
    for h in range(2):
        for s in COVERS[h]:
            queues[h].wait_ge(sem["cast%d" % s], 1)
        queues[h].dma_start(T.y[:, PIECE[h]], T.ys[:, PIECE[h]]).then_inc(sem["out%d" % h], 16)
        queues[h].wait_ge(sem["out%d" % h], 16)
    g.wait_ge(sem.sent, sent[0])
